import numpy as np
import ml_dtypes


def mxq(x, axis, fmt="e4m3"):
    dtype, down = {"e4m3": (ml_dtypes.float8_e4m3fn, 7), "e5m2": (ml_dtypes.float8_e5m2, 14)}[fmt]
    v = np.moveaxis(np.asarray(x, np.float32).astype(ml_dtypes.bfloat16).astype(np.float64), axis, -1)
    blocks = v.reshape(v.shape[:-1] + (-1, 32))
    amax = np.abs(blocks).max(-1, keepdims=True)
    byte = np.maximum(np.where(amax > 0, np.frexp(amax)[1] - 1 + 127, 0) - down, 1)
    scale = np.exp2(byte - 127.0)
    codes = (blocks / scale).astype(np.float32).astype(dtype).astype(np.float64)
    return np.moveaxis((codes * scale).reshape(v.shape), -1, axis)


WIDE = False


def mx_kscale(k):
    if not WIDE:
        return np.ones(k)
    levels = np.array([10, -10, 5, -5, 0])
    if k % 512:
        return np.exp2(np.random.permutation(np.resize(levels, k // 32))).repeat(32)
    a = np.empty((k // 512, 16))
    for p in range(k // 512):
        a[p, :8] = np.random.permutation(np.resize(levels, 8))
        for g in range(8):
            far = levels[np.abs(levels - a[p, g]) >= 10]
            a[p, g + 8] = far[np.random.randint(len(far))]
    return np.exp2(a.ravel()).repeat(32)


BF16 = ml_dtypes.bfloat16


def bf(x):
    return np.asarray(x, np.float32).astype(BF16)


def f64(x):
    return np.asarray(x).astype(np.float64)


B, S, D, M, N, C = 16, 512, 256, 512, 512, 2


def cauchy_parts(om, nu, b):
    de = om[:, None] - nu[None, :]
    w = b[None, :] / (0.25 + de * de)
    gr = 0.5 * w
    gi = -de * w
    return gr, gi


def draw0():
    s, t, r = mx_kscale(S), mx_kscale(M), mx_kscale(N)
    return {"x": bf(np.random.standard_normal((B, S, D)) / s[None, :, None]),
            "p": bf(np.random.standard_normal((M, S)) / np.sqrt(S) * s[None, :] * t[:, None]),
            "om": bf(np.random.uniform(-4.0, 4.0, M)),
            "nu": bf(np.random.uniform(-4.0, 4.0, N)),
            "b": bf(np.random.standard_normal(N) * r),
            "c": bf(np.random.standard_normal((N, D)) * 1.5 / np.sqrt(N) / r[:, None]),
            "q": bf(np.random.standard_normal((C, S, M)) / np.sqrt(M) / t[None, None, :])}


def core(x, p, om, nu, b, c, q):
    gr, gi = cauchy_parts(f64(om), f64(nu), f64(b))
    gr, gi = gr, gi
    cq = mxq(f64(c), 0, "e4m3")
    kr = mxq(gr, 1, "e4m3") @ cq
    ki = mxq(gi, 1, "e4m3") @ cq
    u = mxq(f64(p), 1, "e4m3") @ mxq(f64(x), 1, "e4m3")
    fr = kr[None, :, :] * u
    fi = ki[None, :, :] * u
    qq = mxq(f64(q), 2, "e4m3")
    return (qq[0] @ mxq(fr, 1, "e4m3")) - (qq[1] @ mxq(fi, 1, "e4m3"))


def e4m3fn_bytes(y):
    return np.clip(np.asarray(y, np.float64), -448.0, 448.0).astype(np.float32).astype(ml_dtypes.float8_e4m3fn).view(np.uint8)


def e4m3fn_values(b):
    return np.asarray(b, np.uint8).view(ml_dtypes.float8_e4m3fn).astype(np.float64)


def setup_inputs():
    d = draw0()
    x0 = np.asarray(d['x']).astype(np.float64)
    s = (np.max(np.abs(x0), axis=(0, 2), keepdims=True) / 448.0).astype(np.float32)
    out = {}
    for k, v in d.items():
        if k == 'x':
            out['x_bytes'] = e4m3fn_bytes(x0 / s.astype(np.float64))
            out['x_scale'] = s
        else:
            out[k] = v
    return out


def reference(x_bytes, x_scale, p, om, nu, b, c, q):
    return core(e4m3fn_values(x_bytes) * x_scale.astype(np.float64), p, om, nu, b, c, q)

@@ -1,0 +1,283 @@
+from contextlib import ExitStack
+
+import concourse.mybir as mybir
+from concourse.masks import make_identity
+
+F32 = mybir.dt.float32
+BF16 = mybir.dt.bfloat16
+U32 = mybir.dt.uint32
+U8 = mybir.dt.uint8
+FP8 = mybir.dt.float8_e4m3fn
+FP8X4 = mybir.dt.float8_e4m3fn_x4
+ACT = mybir.ActivationFunctionType
+ALU = mybir.AluOpType
+
+B, S, D, M, N = 16, 512, 256, 512, 512
+P = 128
+T = 4
+HD = D // 2
+
+FLOPS = 2 * B * M * S * D + 2 * 2 * B * S * M * D + 2 * 2 * M * N * D
+
+
+def tile_cauchytransferfunctionfilter_t_kernel(tc, x_bytes, x_scale, p, om, nu, b, c, q, out):
+    nc = tc.nc
+    with ExitStack() as ctx:
+        keep = ctx.enter_context(tc.tile_pool(name="keep", bufs=1))
+        work = ctx.enter_context(tc.tile_pool(name="work", bufs=3))
+        xpool = ctx.enter_context(tc.tile_pool(name="xpool", bufs=4))
+        outs = ctx.enter_context(tc.tile_pool(name="outs", bufs=4))
+        psum = ctx.enter_context(tc.psum_pool(name="psum", bufs=4))
+        ctx.enter_context(tc.manual_schedule())
+
+        nu_sb = keep.tile([P, T], BF16, name="nu_sb")
+        nc.sync.dma_start(out=nu_sb[:], in_=nu.rearrange("(p t) -> p t", t=T))
+        b_sb = keep.tile([P, T], BF16, name="b_sb")
+        nc.sync.dma_start(out=b_sb[:], in_=b.rearrange("(p t) -> p t", t=T))
+        om_sb = keep.tile([P, M], BF16, name="om_sb")
+        nc.sync.dma_start(out=om_sb[:], in_=om.partition_broadcast(P))
+        xs_sb = keep.tile([P, T], F32, name="xs_sb")
+        nc.sync.dma_start(out=xs_sb[:], in_=x_scale.rearrange("o (p t) e -> p (o t e)", t=T))
+
+        x_view = x_bytes.rearrange("b (p t) d -> p b t d", t=T)
+        x_tiles = {}
+
+        def load_x(b0, n):
+            xb = keep.tile([P, n, T, D], U8, name="xb%d" % b0)
+            nc.sync.dma_start(out=xb[:], in_=x_view[:, b0 : b0 + n])
+            for i in range(n):
+                x_tiles[b0 + i] = xb[:, i]
+
+        load_x(0, 2)
+        c_sb = keep.tile([P, T, D], BF16, name="c_sb")
+        nc.sync.dma_start(out=c_sb[:], in_=c.rearrange("(p t) d -> p t d", t=T))
+        p_sb = keep.tile([P, T, S], BF16, name="p_sb")
+        nc.sync.dma_start(out=p_sb[:], in_=p.rearrange("(c t) s -> c t s", t=T))
+        load_x(2, 2)
+        q_sb = []
+        for r in range(2):
+            qr = keep.tile([P, T, M], BF16, name="q_sb%d" % r)
+            nc.sync.dma_start(out=qr[:], in_=q[r].rearrange("(c j) m -> c j m", j=T))
+            q_sb.append(qr)
+        load_x(4, 4)
+        load_x(8, 4)
+        load_x(12, 4)
+
+        warm = keep.tile([P, 1], F32, name="warm")
+        nc.vector.memset(warm[:], 0.0)
+        warm2 = keep.tile([P, 1], F32, name="warm2")
+        nc.scalar.activation(out=warm2[:], in_=warm[:], func=ACT.Square)
+        ident = keep.tile([P, P], F32, name="ident")
+        make_identity(nc, ident[:])
+
+        om_v = om_sb[:].rearrange("p (c t) -> p t c", t=T)
+        deb = keep.tile([P, T, M], F32, name="deb")
+        sq = keep.tile([P, T, M], F32, name="sq")
+        rec = keep.tile([P, T, M], F32, name="rec")
+        for t in range(T):
+            nc.scalar.activation(
+                out=sq[:, t].rearrange("p (a c) -> p a c", a=T), in_=om_v, func=ACT.Square,
+                bias=nu_sb[:, t : t + 1], scale=-1.0,
+            )
+            nc.gpsimd.tensor_scalar(
+                out=deb[:, t].rearrange("p (a c) -> p a c", a=T), in0=om_v,
+                scalar1=nu_sb[:, t : t + 1], scalar2=b_sb[:, t : t + 1], op0=ALU.subtract, op1=ALU.mult,
+            )
+        for t in range(0, T, 2):
+            nc.vector.tensor_scalar(out=sq[:, t : t + 2], in0=sq[:, t : t + 2], scalar1=0.25, scalar2=None, op0=ALU.add)
+            nc.vector.reciprocal(out=rec[:, t : t + 2], in_=sq[:, t : t + 2])
+
+        ci = keep.tile([P, D, T], BF16, name="ci", align_bytes=64)
+        nc.gpsimd.tensor_scalar(
+            out=ci[:], in0=c_sb[:].rearrange("p t d -> p d t"), scalar1=1.0, scalar2=0.0, op0=ALU.mult, op1=ALU.add
+        )
+        cc = keep.tile([P, D], U32, name="cc", align_bytes=64)
+        cs = keep.tile([P, D], U8, name="cs", align_bytes=64)
+
+        def quant(codes, scales, vals):
+            nc.vector.quantize_mx(out=codes.bitcast(FP8X4), scales=scales, in_=vals)
+
+        xw_t, xi_t, xc_t = {}, {}, {}
+
+        def widen(i):
+            xw = xpool.tile([P, T, D], BF16, name="xw")
+            for t in range(T):
+                nc.scalar.activation(
+                    out=xw[:, t], in_=x_tiles[i][:, t].bitcast(FP8), func=ACT.Copy, scale=xs_sb[:, t : t + 1]
+                )
+            xw_t[i] = xw
+
+        def interleave(i):
+            xi = xpool.tile([P, D, T], BF16, name="xi", align_bytes=64)
+            nc.gpsimd.tensor_scalar(
+                out=xi[:], in0=xw_t[i][:].rearrange("p t d -> p d t"), scalar1=1.0, scalar2=0.0,
+                op0=ALU.mult, op1=ALU.add,
+            )
+            xi_t[i] = xi
+
+        def quant_x(i):
+            xc = work.tile([P, D], U32, name="xc", align_bytes=64)
+            xsc = work.tile([P, D], U8, name="xsc", align_bytes=64)
+            quant(xc[:], xsc[:], xi_t[i][:].rearrange("p d t -> p (d t)"))
+            xc_t[i] = (xc, xsc)
+
+        def turn(src, dst):
+            words = src[:].bitcast(F32)
+            dwords = dst[:].rearrange("p c j -> p (c j)").bitcast(F32).rearrange("p (a c u) -> p a c u", a=T, u=2)
+            for a in range(0, T, 2):
+                bank = psum.tile([P, 2, 2, P], F32, name="o")
+                for e in range(2):
+                    for u in range(2):
+                        nc.tensor.transpose(bank[:, e, u], words[:, a + e, u::2], ident[:])
+                nc.scalar.copy(out=dwords[:, a : a + 2], in_=bank[:].rearrange("p a u c -> p a c u"))
+
+        pg = keep.tile([P, M, T], BF16, name="pg", align_bytes=64)
+        pc = keep.tile([P, M], U32, name="pc", align_bytes=64)
+        ps = keep.tile([P, M], U8, name="ps", align_bytes=64)
+        qg, qc, qs = [], [], []
+        for r in range(2):
+            qg_r = keep.tile([P, S, T], BF16, name="qg%d" % r, align_bytes=64)
+            qc_r = keep.tile([P, S], U32, name="qc%d" % r, align_bytes=64)
+            qs_r = keep.tile([P, S], U8, name="qs%d" % r, align_bytes=64)
+            qg.append(qg_r)
+            qc.append(qc_r)
+            qs.append(qs_r)
+
+        widen(0)
+        interleave(0)
+        turn(p_sb, pg)
+        widen(1)
+        interleave(1)
+        turn(q_sb[0], qg[0])
+        turn(q_sb[1], qg[1])
+        widen(2)
+        interleave(2)
+        widen(3)
+        interleave(3)
+
+        quant(cc[:], cs[:], ci[:].rearrange("p d t -> p (d t)"))
+        g = keep.tile([P, 2, 2, M // 2, T], BF16, name="g", align_bytes=64)
+        gc = keep.tile([P, 2, 2, M // 2], U32, name="gc", align_bytes=64)
+        gs = keep.tile([P, 2, 2, M // 2], U8, name="gs", align_bytes=64)
+        for h in range(2):
+            cols = slice(h * M // 2, (h + 1) * M // 2)
+            rec_v = rec[:, :, cols].rearrange("p t m -> p m t")
+            nc.vector.scalar_tensor_tensor(
+                out=g[:, h, 0], in0=rec_v, scalar=0.5,
+                in1=b_sb[:].unsqueeze(1).to_broadcast([P, M // 2, T]), op0=ALU.mult, op1=ALU.mult,
+            )
+            nc.vector.tensor_tensor(
+                out=g[:, h, 1], in0=rec_v, in1=deb[:, :, cols].rearrange("p t m -> p m t"), op=ALU.mult
+            )
+        for h in range(2):
+            quant(
+                gc[:, h].rearrange("p r m -> p (r m)"), gs[:, h].rearrange("p r m -> p (r m)"),
+                g[:, h].rearrange("p r m t -> p (r m t)"),
+            )
+
+        kri = keep.tile([P, 2, 2, HD, T], F32, name="kri")
+        for dh in range(2):
+            for r in range(2):
+                kb = psum.tile([P, T, HD], F32, name="o")
+                for t in range(T):
+                    m0 = (t % 2) * P
+                    nc.tensor.matmul_mx(
+                        out=kb[:, t],
+                        lhsT=gc[:, t // 2, r, m0 : m0 + P].bitcast(FP8X4), lhsT_scale=gs[:, t // 2, r, m0 : m0 + P],
+                        rhs=cc[:, dh * HD : (dh + 1) * HD].bitcast(FP8X4), rhs_scale=cs[:, dh * HD : (dh + 1) * HD],
+                        start=True, stop=True,
+                    )
+                dst = kri[:, dh, r]
+                src = kb[:].rearrange("p t d -> p d t")
+                nc.scalar.copy(out=dst, in_=src)
+        quant(pc[:], ps[:], pg[:].rearrange("p c t -> p (c t)"))
+        quant_x(0)
+        quant_x(1)
+        for r in range(2):
+            quant(qc[r][:], qs[r][:], qg[r][:].rearrange("p c t -> p (c t)"))
+
+        u_t, f_t, fc_t, o_t = {}, {}, {}, {}
+
+        def analyse(i):
+            xc, xsc = xc_t[i]
+            for h in range(2):
+                u = psum.tile([P, T, HD], F32, name="u")
+                for t in range(T):
+                    nc.tensor.matmul_mx(
+                        out=u[:, t],
+                        lhsT=pc[:, t * P : (t + 1) * P].bitcast(FP8X4), lhsT_scale=ps[:, t * P : (t + 1) * P],
+                        rhs=xc[:, h * HD : (h + 1) * HD].bitcast(FP8X4), rhs_scale=xsc[:, h * HD : (h + 1) * HD],
+                        start=True, stop=True,
+                    )
+                u_t[i, h] = u
+
+        def filt(i, h):
+            if h == 0:
+                f = work.tile([P, 2, 2, HD, T], BF16, name="f", align_bytes=64)
+                f_t[i] = f
+            nc.vector.tensor_tensor(
+                out=f_t[i][:, h],
+                in0=u_t[i, h][:].rearrange("p t d -> p d t").unsqueeze(1).to_broadcast([P, 2, HD, T]),
+                in1=kri[:, h], op=ALU.mult,
+            )
+
+        def quant_f(i, halves):
+            if i not in fc_t:
+                fc = work.tile([P, 2, 2, HD], U32, name="fc", align_bytes=64)
+                fs = work.tile([P, 2, 2, HD], U8, name="fs", align_bytes=64)
+                fc_t[i] = (fc, fs)
+            fc, fs = fc_t[i]
+            quant(
+                fc[:, halves].rearrange("p h r d -> p (h r d)"), fs[:, halves].rearrange("p h r d -> p (h r d)"),
+                f_t[i][:, halves].rearrange("p h r d t -> p (h r d t)"),
+            )
+
+        def synth(i, h):
+            fc, fs = fc_t[i]
+            o = psum.tile([P, T, HD], F32, name="o")
+            for j in range(T):
+                for r in range(2):
+                    nc.tensor.matmul_mx(
+                        out=o[:, j],
+                        lhsT=qc[r][:, j * P : (j + 1) * P].bitcast(FP8X4), lhsT_scale=qs[r][:, j * P : (j + 1) * P],
+                        rhs=fc[:, h, r].bitcast(FP8X4), rhs_scale=fs[:, h, r],
+                        start=(r == 0), stop=(r == 1),
+                    )
+            o_t[i, h] = o
+
+        ot_t = {}
+
+        def empty(i, h):
+            if h == 0:
+                ot = outs.tile([P, T, D], F32, name="ot")
+                ot_t[i] = ot
+            nc.scalar.copy(out=ot_t[i][:, :, h * HD : (h + 1) * HD], in_=o_t[i, h][:])
+
+        def store(i):
+            nc.sync.dma_start(out=out[i].rearrange("(c j) d -> c j d", j=T), in_=ot_t[i][:])
+
+        both = slice(0, 2)
+        analyse(0)
+        for i in range(B):
+            if i + 4 < B:
+                widen(i + 4)
+                interleave(i + 4)
+            if i + 1 < B:
+                analyse(i + 1)
+            filt(i, 0)
+            if i > 0:
+                quant_f(i - 1, both)
+                synth(i - 1, 0)
+                synth(i - 1, 1)
+            filt(i, 1)
+            if i + 2 < B:
+                quant_x(i + 2)
+            if i > 0:
+                empty(i - 1, 0)
+                empty(i - 1, 1)
+                store(i - 1)
+        for h in range(2):
+            quant_f(B - 1, slice(h, h + 1))
+            synth(B - 1, h)
+            empty(B - 1, h)
+        store(B - 1)

@@ -63,36 +63,12 @@ def tile_cauchytransferfunctionfilter_t_kernel(tc, x_bytes, x_scale, p, om, nu, 
         load_x(8, 4)
         load_x(12, 4)
 
+        quarter = keep.tile([P, 1], F32, name="quarter")
+        nc.vector.memset(quarter[:], 0.25)
         warm = keep.tile([P, 1], F32, name="warm")
-        nc.vector.memset(warm[:], 0.0)
-        warm2 = keep.tile([P, 1], F32, name="warm2")
-        nc.scalar.activation(out=warm2[:], in_=warm[:], func=ACT.Square)
+        nc.scalar.activation(out=warm[:], in_=quarter[:], func=ACT.Abs_reciprocal_sqrt)
         ident = keep.tile([P, P], F32, name="ident")
         make_identity(nc, ident[:])
-
-        om_v = om_sb[:].rearrange("p (c t) -> p t c", t=T)
-        deb = keep.tile([P, T, M], F32, name="deb")
-        sq = keep.tile([P, T, M], F32, name="sq")
-        rec = keep.tile([P, T, M], F32, name="rec")
-        for t in range(T):
-            nc.scalar.activation(
-                out=sq[:, t].rearrange("p (a c) -> p a c", a=T), in_=om_v, func=ACT.Square,
-                bias=nu_sb[:, t : t + 1], scale=-1.0,
-            )
-            nc.gpsimd.tensor_scalar(
-                out=deb[:, t].rearrange("p (a c) -> p a c", a=T), in0=om_v,
-                scalar1=nu_sb[:, t : t + 1], scalar2=b_sb[:, t : t + 1], op0=ALU.subtract, op1=ALU.mult,
-            )
-        for t in range(0, T, 2):
-            nc.vector.tensor_scalar(out=sq[:, t : t + 2], in0=sq[:, t : t + 2], scalar1=0.25, scalar2=None, op0=ALU.add)
-            nc.vector.reciprocal(out=rec[:, t : t + 2], in_=sq[:, t : t + 2])
-
-        ci = keep.tile([P, D, T], BF16, name="ci", align_bytes=64)
-        nc.gpsimd.tensor_scalar(
-            out=ci[:], in0=c_sb[:].rearrange("p t d -> p d t"), scalar1=1.0, scalar2=0.0, op0=ALU.mult, op1=ALU.add
-        )
-        cc = keep.tile([P, D], U32, name="cc", align_bytes=64)
-        cs = keep.tile([P, D], U8, name="cs", align_bytes=64)
 
         def quant(codes, scales, vals):
             nc.vector.quantize_mx(out=codes.bitcast(FP8X4), scales=scales, in_=vals)
@@ -121,7 +97,7 @@ def tile_cauchytransferfunctionfilter_t_kernel(tc, x_bytes, x_scale, p, om, nu, 
             quant(xc[:], xsc[:], xi_t[i][:].rearrange("p d t -> p (d t)"))
             xc_t[i] = (xc, xsc)
 
-        def turn(src, dst):
+        def turn(src, dst, copy):
             words = src[:].bitcast(F32)
             dwords = dst[:].rearrange("p c j -> p (c j)").bitcast(F32).rearrange("p (a c u) -> p a c u", a=T, u=2)
             for a in range(0, T, 2):
@@ -129,7 +105,7 @@ def tile_cauchytransferfunctionfilter_t_kernel(tc, x_bytes, x_scale, p, om, nu, 
                 for e in range(2):
                     for u in range(2):
                         nc.tensor.transpose(bank[:, e, u], words[:, a + e, u::2], ident[:])
-                nc.scalar.copy(out=dwords[:, a : a + 2], in_=bank[:].rearrange("p a u c -> p a c u"))
+                copy(out=dwords[:, a : a + 2], in_=bank[:].rearrange("p a u c -> p a c u"))
 
         pg = keep.tile([P, M, T], BF16, name="pg", align_bytes=64)
         pc = keep.tile([P, M], U32, name="pc", align_bytes=64)
@@ -143,58 +119,102 @@ def tile_cauchytransferfunctionfilter_t_kernel(tc, x_bytes, x_scale, p, om, nu, 
             qc.append(qc_r)
             qs.append(qs_r)
 
-        widen(0)
-        interleave(0)
-        turn(p_sb, pg)
-        widen(1)
-        interleave(1)
-        turn(q_sb[0], qg[0])
-        turn(q_sb[1], qg[1])
-        widen(2)
-        interleave(2)
-        widen(3)
-        interleave(3)
-
-        quant(cc[:], cs[:], ci[:].rearrange("p d t -> p (d t)"))
-        g = keep.tile([P, 2, 2, M // 2, T], BF16, name="g", align_bytes=64)
-        gc = keep.tile([P, 2, 2, M // 2], U32, name="gc", align_bytes=64)
-        gs = keep.tile([P, 2, 2, M // 2], U8, name="gs", align_bytes=64)
+        MH = M // 2
+        om_v = om_sb[:].rearrange("p (c t) -> p t c", t=T)
+        deb = keep.tile([P, T, M], F32, name="deb")
+        sq = keep.tile([P, T, M], F32, name="sq")
+        rs = keep.tile([P, T, M], F32, name="rs")
+        rec = keep.tile([P, T, M], F32, name="rec")
         for h in range(2):
-            cols = slice(h * M // 2, (h + 1) * M // 2)
+            cols = slice(h * MH, (h + 1) * MH)
+            for t in range(T):
+                nc.scalar.activation(
+                    out=sq[:, t, cols].rearrange("p (a c) -> p a c", a=2), in_=om_v[:, 2 * h : 2 * h + 2],
+                    func=ACT.Square, bias=nu_sb[:, t : t + 1], scale=-1.0,
+                )
+            for t in range(0, T, 2):
+                nc.scalar.activation(
+                    out=rs[:, t : t + 2, cols], in_=sq[:, t : t + 2, cols], func=ACT.Abs_reciprocal_sqrt,
+                    bias=quarter[:],
+                )
+            for t in range(0, T, 2):
+                nc.scalar.activation(out=rec[:, t : t + 2, cols], in_=rs[:, t : t + 2, cols], func=ACT.Square)
+        for t in range(T):
+            nc.vector.tensor_scalar(
+                out=deb[:, t].rearrange("p (a c) -> p a c", a=T), in0=om_v,
+                scalar1=nu_sb[:, t : t + 1], scalar2=b_sb[:, t : t + 1], op0=ALU.subtract, op1=ALU.mult,
+            )
+
+        ci = keep.tile([P, D, T], BF16, name="ci", align_bytes=64)
+        nc.gpsimd.tensor_scalar(
+            out=ci[:], in0=c_sb[:].rearrange("p t d -> p d t"), scalar1=1.0, scalar2=0.0, op0=ALU.mult, op1=ALU.add
+        )
+        cc = keep.tile([P, D], U32, name="cc", align_bytes=64)
+        cs = keep.tile([P, D], U8, name="cs", align_bytes=64)
+
+        turn(p_sb, pg, nc.vector.tensor_copy)
+        for i in range(3):
+            widen(i)
+            interleave(i)
+
+        g = keep.tile([P, 2, 2, MH, T], BF16, name="g", align_bytes=64)
+        gc = keep.tile([P, 2, 2, MH], U32, name="gc", align_bytes=64)
+        gs = keep.tile([P, 2, 2, MH], U8, name="gs", align_bytes=64)
+
+        def cauchy(h):
+            cols = slice(h * MH, (h + 1) * MH)
             rec_v = rec[:, :, cols].rearrange("p t m -> p m t")
             nc.vector.scalar_tensor_tensor(
                 out=g[:, h, 0], in0=rec_v, scalar=0.5,
-                in1=b_sb[:].unsqueeze(1).to_broadcast([P, M // 2, T]), op0=ALU.mult, op1=ALU.mult,
+                in1=b_sb[:].unsqueeze(1).to_broadcast([P, MH, T]), op0=ALU.mult, op1=ALU.mult,
             )
             nc.vector.tensor_tensor(
                 out=g[:, h, 1], in0=rec_v, in1=deb[:, :, cols].rearrange("p t m -> p m t"), op=ALU.mult
             )
-        for h in range(2):
+
+        def quant_g(h):
             quant(
                 gc[:, h].rearrange("p r m -> p (r m)"), gs[:, h].rearrange("p r m -> p (r m)"),
                 g[:, h].rearrange("p r m t -> p (r m t)"),
             )
 
+        k_banks = []
+        for k in range(4):
+            kb = psum.tile([P, T, HD], F32, name="o")
+            k_banks.append(kb)
+
+        def transfer(mh):
+            for dh in range(2):
+                for r in range(2):
+                    for t in range(2):
+                        nc.tensor.matmul_mx(
+                            out=k_banks[2 * dh + r][:, 2 * mh + t],
+                            lhsT=gc[:, mh, r, t * P : (t + 1) * P].bitcast(FP8X4),
+                            lhsT_scale=gs[:, mh, r, t * P : (t + 1) * P],
+                            rhs=cc[:, dh * HD : (dh + 1) * HD].bitcast(FP8X4),
+                            rhs_scale=cs[:, dh * HD : (dh + 1) * HD],
+                            start=True, stop=True,
+                        )
+
+        cauchy(0)
+        quant(pc[:], ps[:], pg[:].rearrange("p c t -> p (c t)"))
+        quant(cc[:], cs[:], ci[:].rearrange("p d t -> p (d t)"))
+        quant_g(0)
+        transfer(0)
+        cauchy(1)
+        quant_x(0)
+        quant_g(1)
+        transfer(1)
+
         kri = keep.tile([P, 2, 2, HD, T], F32, name="kri")
         for dh in range(2):
             for r in range(2):
-                kb = psum.tile([P, T, HD], F32, name="o")
-                for t in range(T):
-                    m0 = (t % 2) * P
-                    nc.tensor.matmul_mx(
-                        out=kb[:, t],
-                        lhsT=gc[:, t // 2, r, m0 : m0 + P].bitcast(FP8X4), lhsT_scale=gs[:, t // 2, r, m0 : m0 + P],
-                        rhs=cc[:, dh * HD : (dh + 1) * HD].bitcast(FP8X4), rhs_scale=cs[:, dh * HD : (dh + 1) * HD],
-                        start=True, stop=True,
-                    )
                 dst = kri[:, dh, r]
-                src = kb[:].rearrange("p t d -> p d t")
-                nc.scalar.copy(out=dst, in_=src)
-        quant(pc[:], ps[:], pg[:].rearrange("p c t -> p (c t)"))
-        quant_x(0)
-        quant_x(1)
-        for r in range(2):
-            quant(qc[r][:], qs[r][:], qg[r][:].rearrange("p c t -> p (c t)"))
+                src = k_banks[2 * dh + r][:].rearrange("p t d -> p d t")
+                if dh == 0 and r == 1:
+                    nc.vector.tensor_copy(out=dst, in_=src)
+                else:
+                    nc.scalar.copy(out=dst, in_=src)
 
         u_t, f_t, fc_t, o_t = {}, {}, {}, {}
 
@@ -217,8 +237,9 @@ def tile_cauchytransferfunctionfilter_t_kernel(tc, x_bytes, x_scale, p, om, nu, 
                 f_t[i] = f
             nc.vector.tensor_tensor(
                 out=f_t[i][:, h],
-                in0=u_t[i, h][:].rearrange("p t d -> p d t").unsqueeze(1).to_broadcast([P, 2, HD, T]),
-                in1=kri[:, h], op=ALU.mult,
+                in0=kri[:, h],
+                in1=u_t[i, h][:].rearrange("p t d -> p d t").unsqueeze(1).to_broadcast([P, 2, HD, T]),
+                op=ALU.mult,
             )
 
         def quant_f(i, halves):
@@ -256,22 +277,27 @@ def tile_cauchytransferfunctionfilter_t_kernel(tc, x_bytes, x_scale, p, om, nu, 
         def store(i):
             nc.sync.dma_start(out=out[i].rearrange("(c j) d -> c j d", j=T), in_=ot_t[i][:])
 
-        both = slice(0, 2)
         analyse(0)
+        for r in range(2):
+            turn(q_sb[r], qg[r], nc.scalar.copy)
+        quant_x(1)
         for i in range(B):
-            if i + 4 < B:
-                widen(i + 4)
-                interleave(i + 4)
+            if i + 3 < B:
+                widen(i + 3)
+                interleave(i + 3)
             if i + 1 < B:
                 analyse(i + 1)
-            filt(i, 0)
-            if i > 0:
-                quant_f(i - 1, both)
-                synth(i - 1, 0)
-                synth(i - 1, 1)
-            filt(i, 1)
             if i + 2 < B:
                 quant_x(i + 2)
+            if i > 0:
+                quant_f(i - 1, slice(0, 2))
+                synth(i - 1, 0)
+                synth(i - 1, 1)
+            filt(i, 0)
+            filt(i, 1)
+            if i == 0:
+                for r in range(2):
+                    quant(qc[r][:], qs[r][:], qg[r][:].rearrange("p c t -> p (c t)"))
             if i > 0:
                 empty(i - 1, 0)
                 empty(i - 1, 1)

@@ -25,7 +25,8 @@ def tile_cauchytransferfunctionfilter_t_kernel(tc, x_bytes, x_scale, p, om, nu, 
     with ExitStack() as ctx:
         keep = ctx.enter_context(tc.tile_pool(name="keep", bufs=1))
         work = ctx.enter_context(tc.tile_pool(name="work", bufs=3))
-        xpool = ctx.enter_context(tc.tile_pool(name="xpool", bufs=4))
+        xpool = ctx.enter_context(tc.tile_pool(name="xpool", bufs=3))
+        ipool = ctx.enter_context(tc.tile_pool(name="ipool", bufs=2))
         outs = ctx.enter_context(tc.tile_pool(name="outs", bufs=4))
         psum = ctx.enter_context(tc.psum_pool(name="psum", bufs=4))
         ctx.enter_context(tc.manual_schedule())
@@ -84,11 +85,22 @@ def tile_cauchytransferfunctionfilter_t_kernel(tc, x_bytes, x_scale, p, om, nu, 
             xw_t[i] = xw
 
         def interleave(i):
-            xi = xpool.tile([P, D, T], BF16, name="xi", align_bytes=64)
+            xi = ipool.tile([P, D, T], BF16, name="xi", align_bytes=64)
             nc.gpsimd.tensor_scalar(
                 out=xi[:], in0=xw_t[i][:].rearrange("p t d -> p d t"), scalar1=1.0, scalar2=0.0,
                 op0=ALU.mult, op1=ALU.add,
             )
+            xi_t[i] = xi
+
+        def widen_and_interleave_on_vector(i):
+            xw = xpool.tile([P, T, D], BF16, name="xw")
+            for t in range(T):
+                nc.vector.tensor_scalar(
+                    out=xw[:, t], in0=x_tiles[i][:, t].bitcast(FP8), scalar1=xs_sb[:, t : t + 1], scalar2=None,
+                    op0=ALU.mult,
+                )
+            xi = ipool.tile([P, D, T], BF16, name="xi", align_bytes=64)
+            nc.vector.tensor_copy(out=xi[:], in_=xw[:].rearrange("p t d -> p d t"))
             xi_t[i] = xi
 
         def quant_x(i):
@@ -152,10 +164,13 @@ def tile_cauchytransferfunctionfilter_t_kernel(tc, x_bytes, x_scale, p, om, nu, 
         cc = keep.tile([P, D], U32, name="cc", align_bytes=64)
         cs = keep.tile([P, D], U8, name="cs", align_bytes=64)
 
+        widen_and_interleave_on_vector(0)
         turn(p_sb, pg, nc.vector.tensor_copy)
-        for i in range(3):
+        quant_x(0)
+        for i in range(1, 4):
             widen(i)
-            interleave(i)
+        interleave(1)
+        interleave(2)
 
         g = keep.tile([P, 2, 2, MH, T], BF16, name="g", align_bytes=64)
         gc = keep.tile([P, 2, 2, MH], U32, name="gc", align_bytes=64)
@@ -202,7 +217,7 @@ def tile_cauchytransferfunctionfilter_t_kernel(tc, x_bytes, x_scale, p, om, nu, 
         quant_g(0)
         transfer(0)
         cauchy(1)
-        quant_x(0)
+        quant_x(1)
         quant_g(1)
         transfer(1)
 
@@ -253,10 +268,10 @@ def tile_cauchytransferfunctionfilter_t_kernel(tc, x_bytes, x_scale, p, om, nu, 
                 f_t[i][:, halves].rearrange("p h r d t -> p (h r d t)"),
             )
 
-        def synth(i, h):
+        def synth(i, h, j0=0, j1=T):
             fc, fs = fc_t[i]
             o = psum.tile([P, T, HD], F32, name="o")
-            for j in range(T):
+            for j in range(j0, j1):
                 for r in range(2):
                     nc.tensor.matmul_mx(
                         out=o[:, j],
@@ -280,15 +295,16 @@ def tile_cauchytransferfunctionfilter_t_kernel(tc, x_bytes, x_scale, p, om, nu, 
         analyse(0)
         for r in range(2):
             turn(q_sb[r], qg[r], nc.scalar.copy)
-        quant_x(1)
+        interleave(3)
         for i in range(B):
-            if i + 3 < B:
-                widen(i + 3)
-                interleave(i + 3)
+            if i + 4 < B:
+                widen(i + 4)
             if i + 1 < B:
                 analyse(i + 1)
             if i + 2 < B:
                 quant_x(i + 2)
+            if i + 4 < B:
+                interleave(i + 4)
             if i > 0:
                 quant_f(i - 1, slice(0, 2))
                 synth(i - 1, 0)
@@ -302,8 +318,13 @@ def tile_cauchytransferfunctionfilter_t_kernel(tc, x_bytes, x_scale, p, om, nu, 
                 empty(i - 1, 0)
                 empty(i - 1, 1)
                 store(i - 1)
-        for h in range(2):
-            quant_f(B - 1, slice(h, h + 1))
-            synth(B - 1, h)
-            empty(B - 1, h)
-        store(B - 1)
+        last = out[B - 1].rearrange("(c j) d -> c j d", j=T)
+        quant_f(B - 1, slice(0, 1))
+        synth(B - 1, 0)
+        empty(B - 1, 0)
+        nc.sync.dma_start(out=last[:, :, :HD], in_=ot_t[B - 1][:, :, :HD])
+        quant_f(B - 1, slice(1, 2))
+        for j0, copy in ((0, nc.scalar.copy), (2, nc.vector.tensor_copy)):
+            synth(B - 1, 1, j0, j0 + 2)
+            copy(out=ot_t[B - 1][:, j0 : j0 + 2, HD:], in_=o_t[B - 1, 1][:, j0 : j0 + 2])
+            nc.sync.dma_start(out=last[:, j0 : j0 + 2, HD:], in_=ot_t[B - 1][:, j0 : j0 + 2, HD:])

@@ -26,19 +26,22 @@ def tile_cauchytransferfunctionfilter_t_kernel(tc, x_bytes, x_scale, p, om, nu, 
         keep = ctx.enter_context(tc.tile_pool(name="keep", bufs=1))
         work = ctx.enter_context(tc.tile_pool(name="work", bufs=3))
         xpool = ctx.enter_context(tc.tile_pool(name="xpool", bufs=3))
-        ipool = ctx.enter_context(tc.tile_pool(name="ipool", bufs=2))
+        ipool = ctx.enter_context(tc.tile_pool(name="ipool", bufs=4))
         outs = ctx.enter_context(tc.tile_pool(name="outs", bufs=4))
         psum = ctx.enter_context(tc.psum_pool(name="psum", bufs=4))
         ctx.enter_context(tc.manual_schedule())
 
+        om_row = keep.tile([P, M], BF16, name="om_row")
+        nc.vector.memset(om_row[:], 0.0)
+        ones = keep.tile([P, P], BF16, name="ones")
+        nc.vector.memset(ones[:], 1.0)
+        nc.sync.dma_start(out=om_row[0:1, :], in_=om.rearrange("(o m) -> o m", o=1))
         nu_sb = keep.tile([P, T], BF16, name="nu_sb")
-        nc.sync.dma_start(out=nu_sb[:], in_=nu.rearrange("(p t) -> p t", t=T))
+        nc.scalar.dma_start(out=nu_sb[:], in_=nu.rearrange("(p t) -> p t", t=T))
         b_sb = keep.tile([P, T], BF16, name="b_sb")
-        nc.sync.dma_start(out=b_sb[:], in_=b.rearrange("(p t) -> p t", t=T))
-        om_sb = keep.tile([P, M], BF16, name="om_sb")
-        nc.sync.dma_start(out=om_sb[:], in_=om.partition_broadcast(P))
+        nc.scalar.dma_start(out=b_sb[:], in_=b.rearrange("(p t) -> p t", t=T))
         xs_sb = keep.tile([P, T], F32, name="xs_sb")
-        nc.sync.dma_start(out=xs_sb[:], in_=x_scale.rearrange("o (p t) e -> p (o t e)", t=T))
+        nc.scalar.dma_start(out=xs_sb[:], in_=x_scale.rearrange("o (p t) e -> p (o t e)", t=T))
 
         x_view = x_bytes.rearrange("b (p t) d -> p b t d", t=T)
         x_tiles = {}
@@ -76,31 +79,27 @@ def tile_cauchytransferfunctionfilter_t_kernel(tc, x_bytes, x_scale, p, om, nu, 
 
         xw_t, xi_t, xc_t = {}, {}, {}
 
-        def widen(i):
+        def widen_plane(copy_engine_is_vector, xw, i, t):
+            src = x_tiles[i][:, t].bitcast(FP8)
+            if copy_engine_is_vector:
+                nc.vector.tensor_scalar(
+                    out=xw[:, t], in0=src, scalar1=xs_sb[:, t : t + 1], scalar2=None, op0=ALU.mult
+                )
+            else:
+                nc.scalar.activation(out=xw[:, t], in_=src, func=ACT.Copy, scale=xs_sb[:, t : t + 1])
+
+        def widen(i, on_vector):
             xw = xpool.tile([P, T, D], BF16, name="xw")
             for t in range(T):
-                nc.scalar.activation(
-                    out=xw[:, t], in_=x_tiles[i][:, t].bitcast(FP8), func=ACT.Copy, scale=xs_sb[:, t : t + 1]
-                )
+                widen_plane(t in on_vector, xw, i, t)
             xw_t[i] = xw
 
-        def interleave(i):
-            xi = ipool.tile([P, D, T], BF16, name="xi", align_bytes=64)
-            nc.gpsimd.tensor_scalar(
-                out=xi[:], in0=xw_t[i][:].rearrange("p t d -> p d t"), scalar1=1.0, scalar2=0.0,
-                op0=ALU.mult, op1=ALU.add,
-            )
-            xi_t[i] = xi
+        def by_fours(dst, src):
+            return {"out": dst.rearrange("p (c i) t -> p c t i", i=4), "in_": src.rearrange("p t (c i) -> p c t i", i=4)}
 
-        def widen_and_interleave_on_vector(i):
-            xw = xpool.tile([P, T, D], BF16, name="xw")
-            for t in range(T):
-                nc.vector.tensor_scalar(
-                    out=xw[:, t], in0=x_tiles[i][:, t].bitcast(FP8), scalar1=xs_sb[:, t : t + 1], scalar2=None,
-                    op0=ALU.mult,
-                )
+        def interleave(i, copy):
             xi = ipool.tile([P, D, T], BF16, name="xi", align_bytes=64)
-            nc.vector.tensor_copy(out=xi[:], in_=xw[:].rearrange("p t d -> p d t"))
+            copy(**by_fours(xi[:], xw_t[i][:]))
             xi_t[i] = xi
 
         def quant_x(i):
@@ -132,7 +131,12 @@ def tile_cauchytransferfunctionfilter_t_kernel(tc, x_bytes, x_scale, p, om, nu, 
             qs.append(qs_r)
 
         MH = M // 2
-        om_v = om_sb[:].rearrange("p (c t) -> p t c", t=T)
+        om_bank = psum.tile([P, M], F32, name="o")
+        nc.tensor.matmul(om_bank[:], lhsT=ones[:], rhs=om_row[:], start=True, stop=True)
+        om_sb = keep.tile([P, M], BF16, name="om_sb")
+        nc.vector.tensor_copy(
+            out=om_sb[:].rearrange("p (t c) -> p t c", t=T), in_=om_bank[:].rearrange("p (c t) -> p t c", t=T)
+        )
         deb = keep.tile([P, T, M], F32, name="deb")
         sq = keep.tile([P, T, M], F32, name="sq")
         rs = keep.tile([P, T, M], F32, name="rs")
@@ -141,8 +145,7 @@ def tile_cauchytransferfunctionfilter_t_kernel(tc, x_bytes, x_scale, p, om, nu, 
             cols = slice(h * MH, (h + 1) * MH)
             for t in range(T):
                 nc.scalar.activation(
-                    out=sq[:, t, cols].rearrange("p (a c) -> p a c", a=2), in_=om_v[:, 2 * h : 2 * h + 2],
-                    func=ACT.Square, bias=nu_sb[:, t : t + 1], scale=-1.0,
+                    out=sq[:, t, cols], in_=om_sb[:, cols], func=ACT.Square, bias=nu_sb[:, t : t + 1], scale=-1.0,
                 )
             for t in range(0, T, 2):
                 nc.scalar.activation(
@@ -153,24 +156,18 @@ def tile_cauchytransferfunctionfilter_t_kernel(tc, x_bytes, x_scale, p, om, nu, 
                 nc.scalar.activation(out=rec[:, t : t + 2, cols], in_=rs[:, t : t + 2, cols], func=ACT.Square)
         for t in range(T):
             nc.vector.tensor_scalar(
-                out=deb[:, t].rearrange("p (a c) -> p a c", a=T), in0=om_v,
+                out=deb[:, t], in0=om_sb[:],
                 scalar1=nu_sb[:, t : t + 1], scalar2=b_sb[:, t : t + 1], op0=ALU.subtract, op1=ALU.mult,
             )
 
         ci = keep.tile([P, D, T], BF16, name="ci", align_bytes=64)
-        nc.gpsimd.tensor_scalar(
-            out=ci[:], in0=c_sb[:].rearrange("p t d -> p d t"), scalar1=1.0, scalar2=0.0, op0=ALU.mult, op1=ALU.add
-        )
+        nc.vector.tensor_copy(**by_fours(ci[:], c_sb[:]))
         cc = keep.tile([P, D], U32, name="cc", align_bytes=64)
         cs = keep.tile([P, D], U8, name="cs", align_bytes=64)
 
-        widen_and_interleave_on_vector(0)
         turn(p_sb, pg, nc.vector.tensor_copy)
-        quant_x(0)
-        for i in range(1, 4):
-            widen(i)
-        interleave(1)
-        interleave(2)
+        widen(1, ())
+        interleave(1, nc.scalar.copy)
 
         g = keep.tile([P, 2, 2, MH, T], BF16, name="g", align_bytes=64)
         gc = keep.tile([P, 2, 2, MH], U32, name="gc", align_bytes=64)
@@ -216,8 +213,10 @@ def tile_cauchytransferfunctionfilter_t_kernel(tc, x_bytes, x_scale, p, om, nu, 
         quant(cc[:], cs[:], ci[:].rearrange("p d t -> p (d t)"))
         quant_g(0)
         transfer(0)
+        widen(0, range(T))
+        interleave(0, nc.vector.tensor_copy)
         cauchy(1)
-        quant_x(1)
+        quant_x(0)
         quant_g(1)
         transfer(1)
 
@@ -226,7 +225,7 @@ def tile_cauchytransferfunctionfilter_t_kernel(tc, x_bytes, x_scale, p, om, nu, 
             for r in range(2):
                 dst = kri[:, dh, r]
                 src = k_banks[2 * dh + r][:].rearrange("p t d -> p d t")
-                if dh == 0 and r == 1:
+                if r == 1:
                     nc.vector.tensor_copy(out=dst, in_=src)
                 else:
                     nc.scalar.copy(out=dst, in_=src)
@@ -293,18 +292,21 @@ def tile_cauchytransferfunctionfilter_t_kernel(tc, x_bytes, x_scale, p, om, nu, 
             nc.sync.dma_start(out=out[i].rearrange("(c j) d -> c j d", j=T), in_=ot_t[i][:])
 
         analyse(0)
+        quant_x(1)
+        widen(2, ())
+        interleave(2, nc.scalar.copy)
         for r in range(2):
             turn(q_sb[r], qg[r], nc.scalar.copy)
-        interleave(3)
+        widen(3, ())
+        interleave(3, nc.scalar.copy)
         for i in range(B):
             if i + 4 < B:
-                widen(i + 4)
+                widen(i + 4, (3,))
+                interleave(i + 4, nc.scalar.copy)
             if i + 1 < B:
                 analyse(i + 1)
             if i + 2 < B:
                 quant_x(i + 2)
-            if i + 4 < B:
-                interleave(i + 4)
             if i > 0:
                 quant_f(i - 1, slice(0, 2))
                 synth(i - 1, 0)

@@ -26,7 +26,8 @@ def tile_cauchytransferfunctionfilter_t_kernel(tc, x_bytes, x_scale, p, om, nu, 
         keep = ctx.enter_context(tc.tile_pool(name="keep", bufs=1))
         work = ctx.enter_context(tc.tile_pool(name="work", bufs=3))
         xpool = ctx.enter_context(tc.tile_pool(name="xpool", bufs=3))
-        ipool = ctx.enter_context(tc.tile_pool(name="ipool", bufs=4))
+        ipool = ctx.enter_context(tc.tile_pool(name="ipool", bufs=2))
+        gpool = ctx.enter_context(tc.tile_pool(name="gpool", bufs=1))
         outs = ctx.enter_context(tc.tile_pool(name="outs", bufs=4))
         psum = ctx.enter_context(tc.psum_pool(name="psum", bufs=4))
         ctx.enter_context(tc.manual_schedule())
@@ -102,6 +103,14 @@ def tile_cauchytransferfunctionfilter_t_kernel(tc, x_bytes, x_scale, p, om, nu, 
             copy(**by_fours(xi[:], xw_t[i][:]))
             xi_t[i] = xi
 
+        def interleave_on_gpsimd(i):
+            xi = gpool.tile([P, D, T], BF16, name="xi_g", align_bytes=64)
+            nc.gpsimd.tensor_scalar(
+                out=xi[:], in0=xw_t[i][:].rearrange("p t d -> p d t"), scalar1=1.0, scalar2=0.0,
+                op0=ALU.mult, op1=ALU.add,
+            )
+            xi_t[i] = xi
+
         def quant_x(i):
             xc = work.tile([P, D], U32, name="xc", align_bytes=64)
             xsc = work.tile([P, D], U8, name="xsc", align_bytes=64)
@@ -165,9 +174,12 @@ def tile_cauchytransferfunctionfilter_t_kernel(tc, x_bytes, x_scale, p, om, nu, 
         cc = keep.tile([P, D], U32, name="cc", align_bytes=64)
         cs = keep.tile([P, D], U8, name="cs", align_bytes=64)
 
+        widen(0, range(T))
+        interleave_on_gpsimd(0)
         turn(p_sb, pg, nc.vector.tensor_copy)
+        for r in range(2):
+            turn(q_sb[r], qg[r], nc.scalar.copy)
         widen(1, ())
-        interleave(1, nc.scalar.copy)
 
         g = keep.tile([P, 2, 2, MH, T], BF16, name="g", align_bytes=64)
         gc = keep.tile([P, 2, 2, MH], U32, name="gc", align_bytes=64)
@@ -209,23 +221,23 @@ def tile_cauchytransferfunctionfilter_t_kernel(tc, x_bytes, x_scale, p, om, nu, 
                         )
 
         cauchy(0)
-        quant(pc[:], ps[:], pg[:].rearrange("p c t -> p (c t)"))
         quant(cc[:], cs[:], ci[:].rearrange("p d t -> p (d t)"))
         quant_g(0)
         transfer(0)
-        widen(0, range(T))
-        interleave(0, nc.vector.tensor_copy)
         cauchy(1)
         quant_x(0)
         quant_g(1)
         transfer(1)
+        quant(pc[:], ps[:], pg[:].rearrange("p c t -> p (c t)"))
+        for r in range(2):
+            quant(qc[r][:], qs[r][:], qg[r][:].rearrange("p c t -> p (c t)"))
 
         kri = keep.tile([P, 2, 2, HD, T], F32, name="kri")
         for dh in range(2):
             for r in range(2):
                 dst = kri[:, dh, r]
                 src = k_banks[2 * dh + r][:].rearrange("p t d -> p d t")
-                if r == 1:
+                if dh == 0 and r == 1:
                     nc.vector.tensor_copy(out=dst, in_=src)
                 else:
                     nc.scalar.copy(out=dst, in_=src)
@@ -245,88 +257,98 @@ def tile_cauchytransferfunctionfilter_t_kernel(tc, x_bytes, x_scale, p, om, nu, 
                     )
                 u_t[i, h] = u
 
-        def filt(i, h):
-            if h == 0:
+        def filt(n):
+            pair, slot = (n + 1) // 2, (n + 1) % 2
+            if pair not in f_t:
                 f = work.tile([P, 2, 2, HD, T], BF16, name="f", align_bytes=64)
-                f_t[i] = f
+                f_t[pair] = f
             nc.vector.tensor_tensor(
-                out=f_t[i][:, h],
-                in0=kri[:, h],
-                in1=u_t[i, h][:].rearrange("p t d -> p d t").unsqueeze(1).to_broadcast([P, 2, HD, T]),
+                out=f_t[pair][:, slot],
+                in0=kri[:, n % 2],
+                in1=u_t[n // 2, n % 2][:].rearrange("p t d -> p d t").unsqueeze(1).to_broadcast([P, 2, HD, T]),
                 op=ALU.mult,
             )
 
-        def quant_f(i, halves):
-            if i not in fc_t:
+        def quant_f(pair, slots):
+            if pair not in fc_t:
                 fc = work.tile([P, 2, 2, HD], U32, name="fc", align_bytes=64)
                 fs = work.tile([P, 2, 2, HD], U8, name="fs", align_bytes=64)
-                fc_t[i] = (fc, fs)
-            fc, fs = fc_t[i]
+                fc_t[pair] = (fc, fs)
+            fc, fs = fc_t[pair]
             quant(
-                fc[:, halves].rearrange("p h r d -> p (h r d)"), fs[:, halves].rearrange("p h r d -> p (h r d)"),
-                f_t[i][:, halves].rearrange("p h r d t -> p (h r d t)"),
+                fc[:, slots].rearrange("p h r d -> p (h r d)"), fs[:, slots].rearrange("p h r d -> p (h r d)"),
+                f_t[pair][:, slots].rearrange("p h r d t -> p (h r d t)"),
             )
 
-        def synth(i, h, j0=0, j1=T):
-            fc, fs = fc_t[i]
+        def synth(n, j0=0, j1=T):
+            pair, slot = (n + 1) // 2, (n + 1) % 2
+            fc, fs = fc_t[pair]
             o = psum.tile([P, T, HD], F32, name="o")
             for j in range(j0, j1):
                 for r in range(2):
                     nc.tensor.matmul_mx(
                         out=o[:, j],
                         lhsT=qc[r][:, j * P : (j + 1) * P].bitcast(FP8X4), lhsT_scale=qs[r][:, j * P : (j + 1) * P],
-                        rhs=fc[:, h, r].bitcast(FP8X4), rhs_scale=fs[:, h, r],
+                        rhs=fc[:, slot, r].bitcast(FP8X4), rhs_scale=fs[:, slot, r],
                         start=(r == 0), stop=(r == 1),
                     )
-            o_t[i, h] = o
+            return o
 
         ot_t = {}
 
-        def empty(i, h):
-            if h == 0:
+        def empty(n, o, copy, j0=0, j1=T):
+            i, h = n // 2, n % 2
+            if i not in ot_t:
                 ot = outs.tile([P, T, D], F32, name="ot")
                 ot_t[i] = ot
-            nc.scalar.copy(out=ot_t[i][:, :, h * HD : (h + 1) * HD], in_=o_t[i, h][:])
+            copy(out=ot_t[i][:, j0:j1, h * HD : (h + 1) * HD], in_=o[:, j0:j1])
 
-        def store(i):
-            nc.sync.dma_start(out=out[i].rearrange("(c j) d -> c j d", j=T), in_=ot_t[i][:])
+        def finish(n):
+            empty(n, synth(n), nc.scalar.copy)
+            if n % 2:
+                i = n // 2
+                nc.sync.dma_start(out=out[i].rearrange("(c j) d -> c j d", j=T), in_=ot_t[i][:])
 
         analyse(0)
-        quant_x(1)
+        interleave(1, nc.scalar.copy)
         widen(2, ())
-        interleave(2, nc.scalar.copy)
-        for r in range(2):
-            turn(q_sb[r], qg[r], nc.scalar.copy)
+        interleave_on_gpsimd(2)
         widen(3, ())
         interleave(3, nc.scalar.copy)
         for i in range(B):
             if i + 4 < B:
-                widen(i + 4, (3,))
-                interleave(i + 4, nc.scalar.copy)
+                widen(i + 4, ())
+                if i % 2:
+                    interleave(i + 4, nc.scalar.copy)
+            filt(2 * i)
+            if i < 2:
+                quant_x(i + 1)
             if i + 1 < B:
                 analyse(i + 1)
-            if i + 2 < B:
-                quant_x(i + 2)
-            if i > 0:
-                quant_f(i - 1, slice(0, 2))
-                synth(i - 1, 0)
-                synth(i - 1, 1)
-            filt(i, 0)
-            filt(i, 1)
+            if i == B - 1:
+                break
+            filt(2 * i + 1)
             if i == 0:
-                for r in range(2):
-                    quant(qc[r][:], qs[r][:], qg[r][:].rearrange("p c t -> p (c t)"))
+                quant_f(0, slice(1, 2))
+            else:
+                quant_f(i, slice(0, 2))
+            if 1 <= i and i + 2 < B:
+                quant_x(i + 2)
+            if i % 2 == 0 and i + 4 < B:
+                interleave_on_gpsimd(i + 4)
             if i > 0:
-                empty(i - 1, 0)
-                empty(i - 1, 1)
-                store(i - 1)
-        last = out[B - 1].rearrange("(c j) d -> c j d", j=T)
+                finish(2 * i - 1)
+            finish(2 * i)
+
         quant_f(B - 1, slice(0, 1))
-        synth(B - 1, 0)
-        empty(B - 1, 0)
-        nc.sync.dma_start(out=last[:, :, :HD], in_=ot_t[B - 1][:, :, :HD])
+        finish(2 * B - 3)
+        filt(2 * B - 1)
         quant_f(B - 1, slice(1, 2))
+        empty(2 * B - 2, synth(2 * B - 2), nc.scalar.copy)
+        last = out[B - 1].rearrange("(c j) d -> c j d", j=T)
+        nc.sync.dma_start(out=last[:, :, :HD], in_=ot_t[B - 1][:, :, :HD])
+        quant_f(B, slice(0, 1))
         for j0, copy in ((0, nc.scalar.copy), (2, nc.vector.tensor_copy)):
-            synth(B - 1, 1, j0, j0 + 2)
-            copy(out=ot_t[B - 1][:, j0 : j0 + 2, HD:], in_=o_t[B - 1, 1][:, j0 : j0 + 2])
+            o = synth(2 * B - 1, j0, j0 + 2)
+            empty(2 * B - 1, o, copy, j0, j0 + 2)
             nc.sync.dma_start(out=last[:, j0 : j0 + 2, HD:], in_=ot_t[B - 1][:, j0 : j0 + 2, HD:])

from contextlib import ExitStack

import concourse.mybir as mybir
from concourse.masks import make_identity

F32 = mybir.dt.float32
BF16 = mybir.dt.bfloat16
U32 = mybir.dt.uint32
U8 = mybir.dt.uint8
FP8 = mybir.dt.float8_e4m3fn
FP8X4 = mybir.dt.float8_e4m3fn_x4
ACT = mybir.ActivationFunctionType
ALU = mybir.AluOpType

B, S, D, M, N = 16, 512, 256, 512, 512
P = 128
T = 4
HD = D // 2

FLOPS = 2 * B * M * S * D + 2 * 2 * B * S * M * D + 2 * 2 * M * N * D


def tile_cauchytransferfunctionfilter_t_kernel(tc, x_bytes, x_scale, p, om, nu, b, c, q, out):
    nc = tc.nc
    with ExitStack() as ctx:
        keep = ctx.enter_context(tc.tile_pool(name="keep", bufs=1))
        work = ctx.enter_context(tc.tile_pool(name="work", bufs=3))
        xpool = ctx.enter_context(tc.tile_pool(name="xpool", bufs=3))
        ipool = ctx.enter_context(tc.tile_pool(name="ipool", bufs=2))
        gpool = ctx.enter_context(tc.tile_pool(name="gpool", bufs=1))
        outs = ctx.enter_context(tc.tile_pool(name="outs", bufs=4))
        psum = ctx.enter_context(tc.psum_pool(name="psum", bufs=4))
        ctx.enter_context(tc.manual_schedule())

        om_row = keep.tile([P, M], BF16, name="om_row")
        nc.vector.memset(om_row[:], 0.0)
        ones = keep.tile([P, P], BF16, name="ones")
        nc.vector.memset(ones[:], 1.0)
        nc.sync.dma_start(out=om_row[0:1, :], in_=om.rearrange("(o m) -> o m", o=1))
        nu_sb = keep.tile([P, T], BF16, name="nu_sb")
        nc.scalar.dma_start(out=nu_sb[:], in_=nu.rearrange("(p t) -> p t", t=T))
        b_sb = keep.tile([P, T], BF16, name="b_sb")
        nc.scalar.dma_start(out=b_sb[:], in_=b.rearrange("(p t) -> p t", t=T))
        xs_sb = keep.tile([P, T], F32, name="xs_sb")
        nc.scalar.dma_start(out=xs_sb[:], in_=x_scale.rearrange("o (p t) e -> p (o t e)", t=T))

        x_view = x_bytes.rearrange("b (p t) d -> p b t d", t=T)
        x_tiles = {}

        def load_x(b0, n):
            xb = keep.tile([P, n, T, D], U8, name="xb%d" % b0)
            nc.sync.dma_start(out=xb[:], in_=x_view[:, b0 : b0 + n])
            for i in range(n):
                x_tiles[b0 + i] = xb[:, i]

        load_x(0, 2)
        c_sb = keep.tile([P, T, D], BF16, name="c_sb")
        nc.sync.dma_start(out=c_sb[:], in_=c.rearrange("(p t) d -> p t d", t=T))
        p_sb = keep.tile([P, T, S], BF16, name="p_sb")
        nc.sync.dma_start(out=p_sb[:], in_=p.rearrange("(c t) s -> c t s", t=T))
        load_x(2, 2)
        q_sb = []
        for r in range(2):
            qr = keep.tile([P, T, M], BF16, name="q_sb%d" % r)
            nc.sync.dma_start(out=qr[:], in_=q[r].rearrange("(c j) m -> c j m", j=T))
            q_sb.append(qr)
        load_x(4, 4)
        load_x(8, 4)
        load_x(12, 4)

        quarter = keep.tile([P, 1], F32, name="quarter")
        nc.vector.memset(quarter[:], 0.25)
        warm = keep.tile([P, 1], F32, name="warm")
        nc.scalar.activation(out=warm[:], in_=quarter[:], func=ACT.Abs_reciprocal_sqrt)
        ident = keep.tile([P, P], F32, name="ident")
        make_identity(nc, ident[:])

        def quant(codes, scales, vals):
            nc.vector.quantize_mx(out=codes.bitcast(FP8X4), scales=scales, in_=vals)

        xw_t, xi_t, xc_t = {}, {}, {}

        def widen_plane(copy_engine_is_vector, xw, i, t):
            src = x_tiles[i][:, t].bitcast(FP8)
            if copy_engine_is_vector:
                nc.vector.tensor_scalar(
                    out=xw[:, t], in0=src, scalar1=xs_sb[:, t : t + 1], scalar2=None, op0=ALU.mult
                )
            else:
                nc.scalar.activation(out=xw[:, t], in_=src, func=ACT.Copy, scale=xs_sb[:, t : t + 1])

        def widen(i, on_vector):
            xw = xpool.tile([P, T, D], BF16, name="xw")
            for t in range(T):
                widen_plane(t in on_vector, xw, i, t)
            xw_t[i] = xw

        def by_fours(dst, src):
            return {"out": dst.rearrange("p (c i) t -> p c t i", i=4), "in_": src.rearrange("p t (c i) -> p c t i", i=4)}

        def interleave(i, copy):
            xi = ipool.tile([P, D, T], BF16, name="xi", align_bytes=64)
            copy(**by_fours(xi[:], xw_t[i][:]))
            xi_t[i] = xi

        def interleave_on_gpsimd(i):
            xi = gpool.tile([P, D, T], BF16, name="xi_g", align_bytes=64)
            nc.gpsimd.tensor_scalar(
                out=xi[:], in0=xw_t[i][:].rearrange("p t d -> p d t"), scalar1=1.0, scalar2=0.0,
                op0=ALU.mult, op1=ALU.add,
            )
            xi_t[i] = xi

        def quant_x(i):
            xc = work.tile([P, D], U32, name="xc", align_bytes=64)
            xsc = work.tile([P, D], U8, name="xsc", align_bytes=64)
            quant(xc[:], xsc[:], xi_t[i][:].rearrange("p d t -> p (d t)"))
            xc_t[i] = (xc, xsc)

        def turn(src, dst, copy):
            words = src[:].bitcast(F32)
            dwords = dst[:].rearrange("p c j -> p (c j)").bitcast(F32).rearrange("p (a c u) -> p a c u", a=T, u=2)
            for a in range(0, T, 2):
                bank = psum.tile([P, 2, 2, P], F32, name="o")
                for e in range(2):
                    for u in range(2):
                        nc.tensor.transpose(bank[:, e, u], words[:, a + e, u::2], ident[:])
                copy(out=dwords[:, a : a + 2], in_=bank[:].rearrange("p a u c -> p a c u"))

        pg = keep.tile([P, M, T], BF16, name="pg", align_bytes=64)
        pc = keep.tile([P, M], U32, name="pc", align_bytes=64)
        ps = keep.tile([P, M], U8, name="ps", align_bytes=64)
        qg, qc, qs = [], [], []
        for r in range(2):
            qg_r = keep.tile([P, S, T], BF16, name="qg%d" % r, align_bytes=64)
            qc_r = keep.tile([P, S], U32, name="qc%d" % r, align_bytes=64)
            qs_r = keep.tile([P, S], U8, name="qs%d" % r, align_bytes=64)
            qg.append(qg_r)
            qc.append(qc_r)
            qs.append(qs_r)

        MH = M // 2
        om_bank = psum.tile([P, M], F32, name="o")
        nc.tensor.matmul(om_bank[:], lhsT=ones[:], rhs=om_row[:], start=True, stop=True)
        om_sb = keep.tile([P, M], BF16, name="om_sb")
        nc.vector.tensor_copy(
            out=om_sb[:].rearrange("p (t c) -> p t c", t=T), in_=om_bank[:].rearrange("p (c t) -> p t c", t=T)
        )
        deb = keep.tile([P, T, M], F32, name="deb")
        sq = keep.tile([P, T, M], F32, name="sq")
        rs = keep.tile([P, T, M], F32, name="rs")
        rec = keep.tile([P, T, M], F32, name="rec")
        for h in range(2):
            cols = slice(h * MH, (h + 1) * MH)
            for t in range(T):
                nc.scalar.activation(
                    out=sq[:, t, cols], in_=om_sb[:, cols], func=ACT.Square, bias=nu_sb[:, t : t + 1], scale=-1.0,
                )
            for t in range(0, T, 2):
                nc.scalar.activation(
                    out=rs[:, t : t + 2, cols], in_=sq[:, t : t + 2, cols], func=ACT.Abs_reciprocal_sqrt,
                    bias=quarter[:],
                )
            for t in range(0, T, 2):
                nc.scalar.activation(out=rec[:, t : t + 2, cols], in_=rs[:, t : t + 2, cols], func=ACT.Square)
        for t in range(T):
            nc.vector.tensor_scalar(
                out=deb[:, t], in0=om_sb[:],
                scalar1=nu_sb[:, t : t + 1], scalar2=b_sb[:, t : t + 1], op0=ALU.subtract, op1=ALU.mult,
            )

        ci = keep.tile([P, D, T], BF16, name="ci", align_bytes=64)
        nc.vector.tensor_copy(**by_fours(ci[:], c_sb[:]))
        cc = keep.tile([P, D], U32, name="cc", align_bytes=64)
        cs = keep.tile([P, D], U8, name="cs", align_bytes=64)

        widen(0, range(T))
        interleave_on_gpsimd(0)
        turn(p_sb, pg, nc.vector.tensor_copy)
        for r in range(2):
            turn(q_sb[r], qg[r], nc.scalar.copy)
        widen(1, ())

        g = keep.tile([P, 2, 2, MH, T], BF16, name="g", align_bytes=64)
        gc = keep.tile([P, 2, 2, MH], U32, name="gc", align_bytes=64)
        gs = keep.tile([P, 2, 2, MH], U8, name="gs", align_bytes=64)

        def cauchy(h):
            cols = slice(h * MH, (h + 1) * MH)
            rec_v = rec[:, :, cols].rearrange("p t m -> p m t")
            nc.vector.scalar_tensor_tensor(
                out=g[:, h, 0], in0=rec_v, scalar=0.5,
                in1=b_sb[:].unsqueeze(1).to_broadcast([P, MH, T]), op0=ALU.mult, op1=ALU.mult,
            )
            nc.vector.tensor_tensor(
                out=g[:, h, 1], in0=rec_v, in1=deb[:, :, cols].rearrange("p t m -> p m t"), op=ALU.mult
            )

        def quant_g(h):
            quant(
                gc[:, h].rearrange("p r m -> p (r m)"), gs[:, h].rearrange("p r m -> p (r m)"),
                g[:, h].rearrange("p r m t -> p (r m t)"),
            )

        k_banks = []
        for k in range(4):
            kb = psum.tile([P, T, HD], F32, name="o")
            k_banks.append(kb)

        def transfer(mh):
            for dh in range(2):
                for r in range(2):
                    for t in range(2):
                        nc.tensor.matmul_mx(
                            out=k_banks[2 * dh + r][:, 2 * mh + t],
                            lhsT=gc[:, mh, r, t * P : (t + 1) * P].bitcast(FP8X4),
                            lhsT_scale=gs[:, mh, r, t * P : (t + 1) * P],
                            rhs=cc[:, dh * HD : (dh + 1) * HD].bitcast(FP8X4),
                            rhs_scale=cs[:, dh * HD : (dh + 1) * HD],
                            start=True, stop=True,
                        )

        cauchy(0)
        quant(cc[:], cs[:], ci[:].rearrange("p d t -> p (d t)"))
        quant_g(0)
        transfer(0)
        cauchy(1)
        quant_x(0)
        quant_g(1)
        transfer(1)
        quant(pc[:], ps[:], pg[:].rearrange("p c t -> p (c t)"))
        for r in range(2):
            quant(qc[r][:], qs[r][:], qg[r][:].rearrange("p c t -> p (c t)"))

        kri = keep.tile([P, 2, 2, HD, T], F32, name="kri")
        for dh in range(2):
            for r in range(2):
                dst = kri[:, dh, r]
                src = k_banks[2 * dh + r][:].rearrange("p t d -> p d t")
                if dh == 0 and r == 1:
                    nc.vector.tensor_copy(out=dst, in_=src)
                else:
                    nc.scalar.copy(out=dst, in_=src)

        u_t, f_t, fc_t, o_t = {}, {}, {}, {}

        def analyse(i):
            xc, xsc = xc_t[i]
            for h in range(2):
                u = psum.tile([P, T, HD], F32, name="u")
                for t in range(T):
                    nc.tensor.matmul_mx(
                        out=u[:, t],
                        lhsT=pc[:, t * P : (t + 1) * P].bitcast(FP8X4), lhsT_scale=ps[:, t * P : (t + 1) * P],
                        rhs=xc[:, h * HD : (h + 1) * HD].bitcast(FP8X4), rhs_scale=xsc[:, h * HD : (h + 1) * HD],
                        start=True, stop=True,
                    )
                u_t[i, h] = u

        def filt(n):
            pair, slot = (n + 1) // 2, (n + 1) % 2
            if pair not in f_t:
                f = work.tile([P, 2, 2, HD, T], BF16, name="f", align_bytes=64)
                f_t[pair] = f
            nc.vector.tensor_tensor(
                out=f_t[pair][:, slot],
                in0=kri[:, n % 2],
                in1=u_t[n // 2, n % 2][:].rearrange("p t d -> p d t").unsqueeze(1).to_broadcast([P, 2, HD, T]),
                op=ALU.mult,
            )

        def quant_f(pair, slots):
            if pair not in fc_t:
                fc = work.tile([P, 2, 2, HD], U32, name="fc", align_bytes=64)
                fs = work.tile([P, 2, 2, HD], U8, name="fs", align_bytes=64)
                fc_t[pair] = (fc, fs)
            fc, fs = fc_t[pair]
            quant(
                fc[:, slots].rearrange("p h r d -> p (h r d)"), fs[:, slots].rearrange("p h r d -> p (h r d)"),
                f_t[pair][:, slots].rearrange("p h r d t -> p (h r d t)"),
            )

        def synth(n, j0=0, j1=T):
            pair, slot = (n + 1) // 2, (n + 1) % 2
            fc, fs = fc_t[pair]
            o = psum.tile([P, T, HD], F32, name="o")
            for j in range(j0, j1):
                for r in range(2):
                    nc.tensor.matmul_mx(
                        out=o[:, j],
                        lhsT=qc[r][:, j * P : (j + 1) * P].bitcast(FP8X4), lhsT_scale=qs[r][:, j * P : (j + 1) * P],
                        rhs=fc[:, slot, r].bitcast(FP8X4), rhs_scale=fs[:, slot, r],
                        start=(r == 0), stop=(r == 1),
                    )
            return o

        ot_t = {}

        def empty(n, o, copy, j0=0, j1=T):
            i, h = n // 2, n % 2
            if i not in ot_t:
                ot = outs.tile([P, T, D], F32, name="ot")
                ot_t[i] = ot
            copy(out=ot_t[i][:, j0:j1, h * HD : (h + 1) * HD], in_=o[:, j0:j1])

        def finish(n):
            empty(n, synth(n), nc.scalar.copy)
            if n % 2:
                i = n // 2
                nc.sync.dma_start(out=out[i].rearrange("(c j) d -> c j d", j=T), in_=ot_t[i][:])

        analyse(0)
        interleave(1, nc.scalar.copy)
        widen(2, ())
        interleave_on_gpsimd(2)
        widen(3, ())
        interleave(3, nc.scalar.copy)
        for i in range(B):
            if i + 4 < B:
                widen(i + 4, ())
                if i % 2:
                    interleave(i + 4, nc.scalar.copy)
            filt(2 * i)
            if i < 2:
                quant_x(i + 1)
            if i + 1 < B:
                analyse(i + 1)
            if i == B - 1:
                break
            filt(2 * i + 1)
            if i == 0:
                quant_f(0, slice(1, 2))
            else:
                quant_f(i, slice(0, 2))
            if 1 <= i and i + 2 < B:
                quant_x(i + 2)
            if i % 2 == 0 and i + 4 < B:
                interleave_on_gpsimd(i + 4)
            if i > 0:
                finish(2 * i - 1)
            finish(2 * i)

        quant_f(B - 1, slice(0, 1))
        finish(2 * B - 3)
        filt(2 * B - 1)
        quant_f(B - 1, slice(1, 2))
        empty(2 * B - 2, synth(2 * B - 2), nc.scalar.copy)
        last = out[B - 1].rearrange("(c j) d -> c j d", j=T)
        nc.sync.dma_start(out=last[:, :, :HD], in_=ot_t[B - 1][:, :, :HD])
        quant_f(B, slice(0, 1))
        for j0, copy in ((0, nc.scalar.copy), (2, nc.vector.tensor_copy)):
            o = synth(2 * B - 1, j0, j0 + 2)
            empty(2 * B - 1, o, copy, j0, j0 + 2)
            nc.sync.dma_start(out=last[:, j0 : j0 + 2, HD:], in_=ot_t[B - 1][:, j0 : j0 + 2, HD:])
